import numpy as np
import ml_dtypes


def mxq(x, axis, fmt="e4m3"):
    dtype, down = {"e4m3": (ml_dtypes.float8_e4m3fn, 7), "e5m2": (ml_dtypes.float8_e5m2, 14)}[fmt]
    v = np.moveaxis(np.asarray(x, np.float32).astype(ml_dtypes.bfloat16).astype(np.float64), axis, -1)
    blocks = v.reshape(v.shape[:-1] + (-1, 32))
    amax = np.abs(blocks).max(-1, keepdims=True)
    byte = np.maximum(np.where(amax > 0, np.frexp(amax)[1] - 1 + 127, 0) - down, 1)
    scale = np.exp2(byte - 127.0)
    codes = (blocks / scale).astype(np.float32).astype(dtype).astype(np.float64)
    return np.moveaxis((codes * scale).reshape(v.shape), -1, axis)


WIDE = False


def mx_kscale(k):
    if not WIDE:
        return np.ones(k)
    levels = np.array([10, -10, 5, -5, 0])
    if k % 512:
        return np.exp2(np.random.permutation(np.resize(levels, k // 32))).repeat(32)
    a = np.empty((k // 512, 16))
    for p in range(k // 512):
        a[p, :8] = np.random.permutation(np.resize(levels, 8))
        for g in range(8):
            far = levels[np.abs(levels - a[p, g]) >= 10]
            a[p, g + 8] = far[np.random.randint(len(far))]
    return np.exp2(a.ravel()).repeat(32)


def f64(x):
    return np.asarray(x).astype(np.float64)


def striped(idx):
    return np.tile(idx.reshape(-1, 16).T, (8, 1)).astype(np.uint16)


def unstriped(offs):
    return offs[:16].T.reshape(-1).astype(np.int64)


def pack_weight(w):
    k, n = w.shape
    w = f64(np.asarray(w, np.float32).astype(ml_dtypes.bfloat16)).reshape(k // 32, 32, n)
    amax = np.abs(w).max(1)
    byte = np.clip(np.where(amax > 0, np.frexp(amax)[1] - 1 + 127 - 7, 1), 1, 254)
    scaled = (w * np.exp2(127.0 - byte)[:, None, :]).reshape(k, n).astype(np.float32)
    words = np.ascontiguousarray(scaled.reshape(k // 512, 128, 4, n).transpose(0, 1, 3, 2)).astype(ml_dtypes.float8_e4m3fn).view(np.uint8)
    return words, np.ascontiguousarray(byte.astype(np.uint8).reshape(k // 512, 16, n))


def unpack_weight(words, scales):
    g, p, n, _ = words.shape
    vals = np.ascontiguousarray(words).view(ml_dtypes.float8_e4m3fn).astype(np.float64) * np.repeat(np.exp2(scales.astype(np.float64) - 127.0), 8, axis=1)[..., None]
    return vals.transpose(0, 1, 3, 2).reshape(g * 512, n)


K, T, S, N, D = 512, 1024, 512, 256, 2
P = 2 ** 7


def setup_inputs():
    n = np.random.standard_normal
    s = mx_kscale(K)[:, None]
    packed_xT = pack_weight(n((K, T)) * s)
    return {
        "x_words": packed_xT[0],
        "x_scales": packed_xT[1],
        "w1": (n((K, N)) / np.sqrt(K) / s).astype(np.float32),
        "wf": (np.tile(np.random.uniform(0.3, 0.7, (D, 1, S)), (1, P, 1))).astype(np.float32),
        "wb": (np.tile(np.random.uniform(0.3, 0.7, (D, 1, S)), (1, P, 1))).astype(np.float32),
        "offs": striped(np.random.permutation(T)[:S]),
        "fwd1": striped(np.random.permutation(S)),
        "bwd1": striped(np.random.permutation(S)),
        "fwd2": striped(np.random.permutation(S)),
        "bwd2": striped(np.random.permutation(S)),
    }


def reference(x_words, x_scales, w1, wf, wb, offs, fwd1, bwd1, fwd2, bwd2):
    xq = unpack_weight(x_words, x_scales)[:, unstriped(offs)]
    y = mxq(f64(w1), 0, "e4m3").T @ xq
    g0 = y[:, unstriped(fwd1)]
    g1 = y[:, unstriped(fwd2)]
    p1 = g0 * f64(wf)[0, :1] + g1 * f64(wf)[1, :1]
    p0 = p1[:, unstriped(bwd1)] * f64(wb)[0, :1] + p1[:, unstriped(bwd2)] * f64(wb)[1, :1]
    return p1 + 0.5 * (y - p0)

@@ -1,0 +1,156 @@
+from contextlib import ExitStack
+
+import concourse.mybir as mybir
+
+K, T, S, N = 512, 1024, 512, 256
+FLOPS = 2 * K * N * S
+
+F32 = mybir.dt.float32
+BF16 = mybir.dt.bfloat16
+I32 = mybir.dt.int32
+U32 = mybir.dt.uint32
+U16 = mybir.dt.uint16
+U8 = mybir.dt.uint8
+FP8X4 = mybir.dt.float8_e4m3fn_x4
+MULT = mybir.AluOpType.mult
+ADD = mybir.AluOpType.add
+COPY = mybir.ActivationFunctionType.Copy
+
+P = 128
+PACK = 4
+HALF = S // 2
+SPARE = 16
+GROUP = 16
+
+
+def tile_picked_ymaccor_free_p_kernel(
+    tc, x_words, x_scales, w1, wf, wb, offs, fwd1, bwd1, fwd2, bwd2, out
+):
+    nc = tc.nc
+    with ExitStack() as ctx:
+        lists = ctx.enter_context(tc.tile_pool(name="lists", bufs=1))
+        sb = ctx.enter_context(tc.tile_pool(name="sb", bufs=1))
+        psum = ctx.enter_context(tc.psum_pool(name="psum", bufs=1))
+
+        def load_list(src, name):
+            tile = lists.tile([P, S // GROUP], U16, name=name)
+            nc.sync.dma_start(tile[:], src)
+            return tile
+
+        table_scales = sb.tile([P, T], U8, name="table_scales")
+        for q in range(4):
+            nc.scalar.dma_start(
+                table_scales[32 * q : 32 * q + 32, :].bitcast(I32),
+                x_scales[0, 4 * q : 4 * q + 4, :].bitcast(I32).unsqueeze(0).broadcast_to([8, 4, T // 4]),
+            )
+
+        idx = load_list(offs, "idx")
+        w_view = w1.rearrange("(p j) n -> p j n", j=PACK)
+        w_raw = [sb.tile([P, PACK, P], F32, name="w_raw%d" % b) for b in range(2)]
+        nc.sync.dma_start(w_raw[0][:], w_view[:, :, 0:P])
+        table_words = sb.tile([P, T], I32, name="table_words")
+        nc.sync.dma_start(table_words[:], x_words[0].rearrange("p c r -> p (c r)").bitcast(I32))
+        nc.sync.dma_start(w_raw[1][:], w_view[:, :, P : 2 * P])
+        fwd = [load_list(fwd1, "fwd1"), load_list(fwd2, "fwd2")]
+        wf_all = sb.tile([P, 2, S], F32, name="wf_all")
+        wb_all = sb.tile([P, 2, S], F32, name="wb_all")
+        nc.sync.dma_start(wf_all[:], wf.rearrange("d p s -> p d s"))
+        bwd = [load_list(bwd1, "bwd1"), load_list(bwd2, "bwd2")]
+        nc.sync.dma_start(wb_all[:], wb.rearrange("d p s -> p d s"))
+        wf_sb = [wf_all[:, d, :] for d in range(2)]
+        wb_sb = [wb_all[:, d, :] for d in range(2)]
+
+        y = [sb.tile([P, S + SPARE], F32, name="y%d" % b) for b in range(2)]
+        p1 = [sb.tile([P, S + SPARE], F32, name="p1_%d" % b) for b in range(2)]
+        for window in y + p1:
+            nc.gpsimd.memset(window[:, S:], 0.0)
+
+        picked_scales = sb.tile([P, S], U8, name="picked_scales", align_bytes=64)
+        nc.vector.tensor_copy(picked_scales[:], table_scales[:].indirect(idx[:]))
+
+        w_codes, w_scales = [], []
+        picked_words = []
+        for b in range(2):
+            grouped = sb.tile([P, P, PACK], BF16, name="grouped%d" % b, align_bytes=64)
+            nc.scalar.copy(grouped[:], w_raw[b][:].rearrange("p j n -> p n j"))
+            codes = sb.tile([P, P], U32, name="w_codes%d" % b, align_bytes=64)
+            scales = sb.tile([P, P], U8, name="w_scales%d" % b, align_bytes=64)
+            nc.vector.quantize_mx(
+                out=codes[:].bitcast(FP8X4), scales=scales[:], in_=grouped[:].rearrange("p n j -> p (n j)")
+            )
+            w_codes.append(codes)
+            w_scales.append(scales)
+            if b == 0:
+                for h in range(2):
+                    words = sb.tile([P, HALF], U32, name="picked_words%d" % h, align_bytes=64)
+                    cols = slice(h * HALF // GROUP, (h + 1) * HALF // GROUP)
+                    nc.vector.tensor_copy(words[:], table_words[:].bitcast(U32).indirect(idx[:, cols]))
+                    picked_words.append(words)
+
+        for b in range(2):
+            for h in range(2):
+                acc = psum.tile([P, HALF], F32, name="acc%d%d" % (b, h))
+                nc.tensor.matmul_mx(
+                    out=acc[:],
+                    lhsT=w_codes[b][:].bitcast(FP8X4),
+                    lhsT_scale=w_scales[b][:],
+                    rhs=picked_words[h][:].bitcast(FP8X4),
+                    rhs_scale=picked_scales[:, h * HALF : (h + 1) * HALF],
+                    start=True,
+                    stop=True,
+                )
+                if b == 0:
+                    nc.scalar.copy(y[b][:, h * HALF : (h + 1) * HALF], acc[:])
+                else:
+                    nc.vector.tensor_copy(y[b][:, h * HALF : (h + 1) * HALF], acc[:])
+
+        def fresh(name):
+            return sb.tile([P, S], F32, name=name)
+
+        def fetch(window, offsets, name):
+            got = fresh(name)
+            nc.scalar.activation(got[:], window[:].indirect(offsets[:]), COPY)
+            return got
+
+        def times(a, b, name):
+            prod = fresh(name)
+            nc.vector.tensor_tensor(prod[:], a, b, MULT)
+            return prod
+
+        g00 = fetch(y[0], fwd[0], "g00")
+        a1 = times(y[1][:].indirect(fwd[0][:]), wf_sb[0], "a1")
+        g01 = fetch(y[0], fwd[1], "g01")
+        a0 = times(g00[:], wf_sb[0], "a0")
+        g11 = fetch(y[1], fwd[1], "g11")
+        b0 = times(g01[:], wf_sb[1], "b0")
+        nc.vector.tensor_tensor(p1[0][:, :S], a0[:], b0[:], ADD)
+        b1 = times(g11[:], wf_sb[1], "b1")
+        base0 = fresh("base0")
+        nc.vector.scalar_tensor_tensor(base0[:], y[0][:, :S], 0.5, p1[0][:, :S], MULT, ADD)
+        nc.vector.tensor_tensor(p1[1][:, :S], a1[:], b1[:], ADD)
+        h00 = fetch(p1[0], bwd[0], "h00")
+        h01 = fetch(p1[0], bwd[1], "h01")
+        h10 = fetch(p1[1], bwd[0], "h10")
+        c0 = times(h00[:], wb_sb[0], "c0")
+        base1 = fresh("base1")
+        nc.vector.scalar_tensor_tensor(base1[:], y[1][:, :S], 0.5, p1[1][:, :S], MULT, ADD)
+        t0 = fresh("t0")
+        nc.vector.scalar_tensor_tensor(t0[:], c0[:], -0.5, base0[:], MULT, ADD)
+        d0 = times(h01[:], wb_sb[1], "d0")
+        c1 = times(h10[:], wb_sb[0], "c1")
+        o0 = fresh("o0")
+        nc.vector.scalar_tensor_tensor(o0[:], d0[:], -0.5, t0[:], MULT, ADD)
+        nc.sync.dma_start(out[0:P, :], o0[:])
+        t1 = fresh("t1")
+        nc.vector.scalar_tensor_tensor(t1[:], c1[:], -0.5, base1[:], MULT, ADD)
+        for h in range(2):
+            cols = slice(h * HALF, (h + 1) * HALF)
+            got = sb.tile([P, HALF], F32, name="h11_%d" % h)
+            nc.scalar.activation(
+                got[:], p1[1][:].indirect(bwd[1][:, h * HALF // GROUP : (h + 1) * HALF // GROUP]), COPY
+            )
+            d1 = sb.tile([P, HALF], F32, name="d1_%d" % h)
+            nc.vector.tensor_tensor(d1[:], got[:], wb_sb[1][:, cols], MULT)
+            o1 = sb.tile([P, HALF], F32, name="o1_%d" % h)
+            nc.vector.scalar_tensor_tensor(o1[:], d1[:], -0.5, t1[:, cols], MULT, ADD)
+            nc.sync.dma_start(out[P : 2 * P, cols], o1[:])

@@ -39,7 +39,8 @@ def tile_picked_ymaccor_free_p_kernel(
 
         table_scales = sb.tile([P, T], U8, name="table_scales")
         for q in range(4):
-            nc.scalar.dma_start(
+            queue = nc.scalar if q < 2 else nc.sync
+            queue.dma_start(
                 table_scales[32 * q : 32 * q + 32, :].bitcast(I32),
                 x_scales[0, 4 * q : 4 * q + 4, :].bitcast(I32).unsqueeze(0).broadcast_to([8, 4, T // 4]),
             )
@@ -52,12 +53,12 @@ def tile_picked_ymaccor_free_p_kernel(
         nc.sync.dma_start(table_words[:], x_words[0].rearrange("p c r -> p (c r)").bitcast(I32))
         nc.sync.dma_start(w_raw[1][:], w_view[:, :, P : 2 * P])
         fwd = [load_list(fwd1, "fwd1"), load_list(fwd2, "fwd2")]
-        wf_all = sb.tile([P, 2, S], F32, name="wf_all")
+        wf_sb = [sb.tile([P, S], F32, name="wf%d" % d)[:] for d in range(2)]
         wb_all = sb.tile([P, 2, S], F32, name="wb_all")
-        nc.sync.dma_start(wf_all[:], wf.rearrange("d p s -> p d s"))
+        for d in range(2):
+            nc.sync.dma_start(wf_sb[d], wf[d])
         bwd = [load_list(bwd1, "bwd1"), load_list(bwd2, "bwd2")]
         nc.sync.dma_start(wb_all[:], wb.rearrange("d p s -> p d s"))
-        wf_sb = [wf_all[:, d, :] for d in range(2)]
         wb_sb = [wb_all[:, d, :] for d in range(2)]
 
         y = [sb.tile([P, S + SPARE], F32, name="y%d" % b) for b in range(2)]
@@ -99,7 +100,7 @@ def tile_picked_ymaccor_free_p_kernel(
                     start=True,
                     stop=True,
                 )
-                if b == 0:
+                if h == 0:
                     nc.scalar.copy(y[b][:, h * HALF : (h + 1) * HALF], acc[:])
                 else:
                     nc.vector.tensor_copy(y[b][:, h * HALF : (h + 1) * HALF], acc[:])
@@ -117,16 +118,16 @@ def tile_picked_ymaccor_free_p_kernel(
             nc.vector.tensor_tensor(prod[:], a, b, MULT)
             return prod
 
-        g00 = fetch(y[0], fwd[0], "g00")
-        a1 = times(y[1][:].indirect(fwd[0][:]), wf_sb[0], "a1")
         g01 = fetch(y[0], fwd[1], "g01")
-        a0 = times(g00[:], wf_sb[0], "a0")
-        g11 = fetch(y[1], fwd[1], "g11")
+        a0 = times(y[0][:].indirect(fwd[0][:]), wf_sb[0], "a0")
+        g10 = fetch(y[1], fwd[0], "g10")
         b0 = times(g01[:], wf_sb[1], "b0")
+        g11 = fetch(y[1], fwd[1], "g11")
         nc.vector.tensor_tensor(p1[0][:, :S], a0[:], b0[:], ADD)
-        b1 = times(g11[:], wf_sb[1], "b1")
+        a1 = times(g10[:], wf_sb[0], "a1")
         base0 = fresh("base0")
         nc.vector.scalar_tensor_tensor(base0[:], y[0][:, :S], 0.5, p1[0][:, :S], MULT, ADD)
+        b1 = times(g11[:], wf_sb[1], "b1")
         nc.vector.tensor_tensor(p1[1][:, :S], a1[:], b1[:], ADD)
         h00 = fetch(p1[0], bwd[0], "h00")
         h01 = fetch(p1[0], bwd[1], "h01")

@@ -100,7 +100,7 @@ def tile_picked_ymaccor_free_p_kernel(
                     start=True,
                     stop=True,
                 )
-                if h == 0:
+                if h == 0 or b == 1:
                     nc.scalar.copy(y[b][:, h * HALF : (h + 1) * HALF], acc[:])
                 else:
                     nc.vector.tensor_copy(y[b][:, h * HALF : (h + 1) * HALF], acc[:])
@@ -118,10 +118,9 @@ def tile_picked_ymaccor_free_p_kernel(
             nc.vector.tensor_tensor(prod[:], a, b, MULT)
             return prod
 
-        g01 = fetch(y[0], fwd[1], "g01")
         a0 = times(y[0][:].indirect(fwd[0][:]), wf_sb[0], "a0")
         g10 = fetch(y[1], fwd[0], "g10")
-        b0 = times(g01[:], wf_sb[1], "b0")
+        b0 = times(y[0][:].indirect(fwd[1][:]), wf_sb[1], "b0")
         g11 = fetch(y[1], fwd[1], "g11")
         nc.vector.tensor_tensor(p1[0][:, :S], a0[:], b0[:], ADD)
         a1 = times(g10[:], wf_sb[0], "a1")

from contextlib import ExitStack

import concourse.mybir as mybir

K, T, S, N = 512, 1024, 512, 256
FLOPS = 2 * K * N * S

F32 = mybir.dt.float32
BF16 = mybir.dt.bfloat16
I32 = mybir.dt.int32
U32 = mybir.dt.uint32
U16 = mybir.dt.uint16
U8 = mybir.dt.uint8
FP8X4 = mybir.dt.float8_e4m3fn_x4
MULT = mybir.AluOpType.mult
ADD = mybir.AluOpType.add
COPY = mybir.ActivationFunctionType.Copy

P = 128
PACK = 4
HALF = S // 2
SPARE = 16
GROUP = 16


def tile_picked_ymaccor_free_p_kernel(
    tc, x_words, x_scales, w1, wf, wb, offs, fwd1, bwd1, fwd2, bwd2, out
):
    nc = tc.nc
    with ExitStack() as ctx:
        lists = ctx.enter_context(tc.tile_pool(name="lists", bufs=1))
        sb = ctx.enter_context(tc.tile_pool(name="sb", bufs=1))
        psum = ctx.enter_context(tc.psum_pool(name="psum", bufs=1))

        def load_list(src, name):
            tile = lists.tile([P, S // GROUP], U16, name=name)
            nc.sync.dma_start(tile[:], src)
            return tile

        table_scales = sb.tile([P, T], U8, name="table_scales")
        for q in range(4):
            queue = nc.scalar if q < 2 else nc.sync
            queue.dma_start(
                table_scales[32 * q : 32 * q + 32, :].bitcast(I32),
                x_scales[0, 4 * q : 4 * q + 4, :].bitcast(I32).unsqueeze(0).broadcast_to([8, 4, T // 4]),
            )

        idx = load_list(offs, "idx")
        w_view = w1.rearrange("(p j) n -> p j n", j=PACK)
        w_raw = [sb.tile([P, PACK, P], F32, name="w_raw%d" % b) for b in range(2)]
        nc.sync.dma_start(w_raw[0][:], w_view[:, :, 0:P])
        table_words = sb.tile([P, T], I32, name="table_words")
        nc.sync.dma_start(table_words[:], x_words[0].rearrange("p c r -> p (c r)").bitcast(I32))
        nc.sync.dma_start(w_raw[1][:], w_view[:, :, P : 2 * P])
        fwd = [load_list(fwd1, "fwd1"), load_list(fwd2, "fwd2")]
        wf_sb = [sb.tile([P, S], F32, name="wf%d" % d)[:] for d in range(2)]
        wb_all = sb.tile([P, 2, S], F32, name="wb_all")
        for d in range(2):
            nc.sync.dma_start(wf_sb[d], wf[d])
        bwd = [load_list(bwd1, "bwd1"), load_list(bwd2, "bwd2")]
        nc.sync.dma_start(wb_all[:], wb.rearrange("d p s -> p d s"))
        wb_sb = [wb_all[:, d, :] for d in range(2)]

        y = [sb.tile([P, S + SPARE], F32, name="y%d" % b) for b in range(2)]
        p1 = [sb.tile([P, S + SPARE], F32, name="p1_%d" % b) for b in range(2)]
        for window in y + p1:
            nc.gpsimd.memset(window[:, S:], 0.0)

        picked_scales = sb.tile([P, S], U8, name="picked_scales", align_bytes=64)
        nc.vector.tensor_copy(picked_scales[:], table_scales[:].indirect(idx[:]))

        w_codes, w_scales = [], []
        picked_words = []
        for b in range(2):
            grouped = sb.tile([P, P, PACK], BF16, name="grouped%d" % b, align_bytes=64)
            nc.scalar.copy(grouped[:], w_raw[b][:].rearrange("p j n -> p n j"))
            codes = sb.tile([P, P], U32, name="w_codes%d" % b, align_bytes=64)
            scales = sb.tile([P, P], U8, name="w_scales%d" % b, align_bytes=64)
            nc.vector.quantize_mx(
                out=codes[:].bitcast(FP8X4), scales=scales[:], in_=grouped[:].rearrange("p n j -> p (n j)")
            )
            w_codes.append(codes)
            w_scales.append(scales)
            if b == 0:
                for h in range(2):
                    words = sb.tile([P, HALF], U32, name="picked_words%d" % h, align_bytes=64)
                    cols = slice(h * HALF // GROUP, (h + 1) * HALF // GROUP)
                    nc.vector.tensor_copy(words[:], table_words[:].bitcast(U32).indirect(idx[:, cols]))
                    picked_words.append(words)

        for b in range(2):
            for h in range(2):
                acc = psum.tile([P, HALF], F32, name="acc%d%d" % (b, h))
                nc.tensor.matmul_mx(
                    out=acc[:],
                    lhsT=w_codes[b][:].bitcast(FP8X4),
                    lhsT_scale=w_scales[b][:],
                    rhs=picked_words[h][:].bitcast(FP8X4),
                    rhs_scale=picked_scales[:, h * HALF : (h + 1) * HALF],
                    start=True,
                    stop=True,
                )
                if h == 0 or b == 1:
                    nc.scalar.copy(y[b][:, h * HALF : (h + 1) * HALF], acc[:])
                else:
                    nc.vector.tensor_copy(y[b][:, h * HALF : (h + 1) * HALF], acc[:])

        def fresh(name):
            return sb.tile([P, S], F32, name=name)

        def fetch(window, offsets, name):
            got = fresh(name)
            nc.scalar.activation(got[:], window[:].indirect(offsets[:]), COPY)
            return got

        def times(a, b, name):
            prod = fresh(name)
            nc.vector.tensor_tensor(prod[:], a, b, MULT)
            return prod

        a0 = times(y[0][:].indirect(fwd[0][:]), wf_sb[0], "a0")
        g10 = fetch(y[1], fwd[0], "g10")
        b0 = times(y[0][:].indirect(fwd[1][:]), wf_sb[1], "b0")
        g11 = fetch(y[1], fwd[1], "g11")
        nc.vector.tensor_tensor(p1[0][:, :S], a0[:], b0[:], ADD)
        a1 = times(g10[:], wf_sb[0], "a1")
        base0 = fresh("base0")
        nc.vector.scalar_tensor_tensor(base0[:], y[0][:, :S], 0.5, p1[0][:, :S], MULT, ADD)
        b1 = times(g11[:], wf_sb[1], "b1")
        nc.vector.tensor_tensor(p1[1][:, :S], a1[:], b1[:], ADD)
        h00 = fetch(p1[0], bwd[0], "h00")
        h01 = fetch(p1[0], bwd[1], "h01")
        h10 = fetch(p1[1], bwd[0], "h10")
        c0 = times(h00[:], wb_sb[0], "c0")
        base1 = fresh("base1")
        nc.vector.scalar_tensor_tensor(base1[:], y[1][:, :S], 0.5, p1[1][:, :S], MULT, ADD)
        t0 = fresh("t0")
        nc.vector.scalar_tensor_tensor(t0[:], c0[:], -0.5, base0[:], MULT, ADD)
        d0 = times(h01[:], wb_sb[1], "d0")
        c1 = times(h10[:], wb_sb[0], "c1")
        o0 = fresh("o0")
        nc.vector.scalar_tensor_tensor(o0[:], d0[:], -0.5, t0[:], MULT, ADD)
        nc.sync.dma_start(out[0:P, :], o0[:])
        t1 = fresh("t1")
        nc.vector.scalar_tensor_tensor(t1[:], c1[:], -0.5, base1[:], MULT, ADD)
        for h in range(2):
            cols = slice(h * HALF, (h + 1) * HALF)
            got = sb.tile([P, HALF], F32, name="h11_%d" % h)
            nc.scalar.activation(
                got[:], p1[1][:].indirect(bwd[1][:, h * HALF // GROUP : (h + 1) * HALF // GROUP]), COPY
            )
            d1 = sb.tile([P, HALF], F32, name="d1_%d" % h)
            nc.vector.tensor_tensor(d1[:], got[:], wb_sb[1][:, cols], MULT)
            o1 = sb.tile([P, HALF], F32, name="o1_%d" % h)
            nc.vector.scalar_tensor_tensor(o1[:], d1[:], -0.5, t1[:, cols], MULT, ADD)
            nc.sync.dma_start(out[P : 2 * P, cols], o1[:])
